import numpy as np
import ml_dtypes


def mxq(x, axis, fmt="e4m3"):
    dtype, down = {"e4m3": (ml_dtypes.float8_e4m3fn, 7), "e5m2": (ml_dtypes.float8_e5m2, 14)}[fmt]
    v = np.moveaxis(np.asarray(x, np.float32).astype(ml_dtypes.bfloat16).astype(np.float64), axis, -1)
    blocks = v.reshape(v.shape[:-1] + (-1, 32))
    amax = np.abs(blocks).max(-1, keepdims=True)
    byte = np.maximum(np.where(amax > 0, np.frexp(amax)[1] - 1 + 127, 0) - down, 1)
    scale = np.exp2(byte - 127.0)
    codes = (blocks / scale).astype(np.float32).astype(dtype).astype(np.float64)
    return np.moveaxis((codes * scale).reshape(v.shape), -1, axis)


WIDE = False


def mx_kscale(k):
    if not WIDE:
        return np.ones(k)
    levels = np.array([10, -10, 5, -5, 0])
    if k % 512:
        return np.exp2(np.random.permutation(np.resize(levels, k // 32))).repeat(32)
    a = np.empty((k // 512, 16))
    for p in range(k // 512):
        a[p, :8] = np.random.permutation(np.resize(levels, 8))
        for g in range(8):
            far = levels[np.abs(levels - a[p, g]) >= 10]
            a[p, g + 8] = far[np.random.randint(len(far))]
    return np.exp2(a.ravel()).repeat(32)


def f64(x):
    return np.asarray(x).astype(np.float64)


def striped(idx):
    return np.tile(idx.reshape(-1, 16).T, (8, 1)).astype(np.uint16)


def unstriped(offs):
    return offs[:16].T.reshape(-1).astype(np.int64)


E2M1 = np.array([0.0, 0.5, 1.0, 1.5, 2.0, 3.0, 4.0, 6.0, -0.0, -0.5, -1.0, -1.5, -2.0, -3.0, -4.0, -6.0])


def pack_weight(w, fmt):
    k, n = w.shape
    w = f64(np.asarray(w, np.float32).astype(ml_dtypes.bfloat16)).reshape(k // 32, 32, n)
    amax = np.abs(w).max(1)
    if fmt == "e4m3":
        byte = np.frexp(amax)[1] - 1 + 127 - 7
    else:
        mant, ex = np.frexp(amax / 6.0)
        byte = np.where(mant > 0.5, ex, ex - 1) + 127
    byte = np.clip(np.where(amax > 0, byte, 1), 1, 254)
    scaled = (w * np.exp2(127.0 - byte)[:, None, :]).reshape(k, n).astype(np.float32)
    by_word = np.ascontiguousarray(scaled.reshape(k // 512, 128, 4, n).transpose(0, 1, 3, 2))
    if fmt == "e4m3":
        words = by_word.astype(ml_dtypes.float8_e4m3fn).view(np.uint8)
    else:
        c = by_word.astype(ml_dtypes.float4_e2m1fn).view(np.uint8) & 0xF
        words = (c[..., 0::2] | (c[..., 1::2] << 4)).reshape(k // 512, 128, 2 * n)
    return np.ascontiguousarray(words), np.ascontiguousarray(byte.astype(np.uint8).reshape(k // 512, 16, n))


def unpack_weight(words, scales, fmt):
    g, _, n = scales.shape
    words = np.ascontiguousarray(words).reshape(g, 128, n, -1)
    if fmt == "e4m3":
        vals = words.view(ml_dtypes.float8_e4m3fn).astype(np.float64)
    else:
        nib = np.empty((g, 128, n, 4), np.uint8)
        nib[..., 0::2] = words & 0xF
        nib[..., 1::2] = words >> 4
        vals = E2M1[nib]
    vals = vals * np.repeat(np.exp2(scales.astype(np.float64) - 127.0), 8, axis=1)[..., None]
    return vals.transpose(0, 1, 3, 2).reshape(g * 512, n)


def gelu(v):
    return 0.5 * v * (1.0 + np.tanh(np.sqrt(2.0 / np.pi) * (v + 0.044715 * v**3)))


K, T, S, P, H, N = 1024, 4096, 1024, 512, 512, 768

def setup_inputs():
    n = np.random.standard_normal
    s = mx_kscale(K)[:, None]
    u = mx_kscale(H)[:, None]
    tab_words, tab_scales = pack_weight(n((K, T)) * s, "e4m3")
    w1 = (0.9 * n((K, H)) / s / np.sqrt(K)).astype(np.float32)
    w2_words, w2_scales = pack_weight(0.9 * n((K, H)) / s / np.sqrt(K), "e2m1")
    w3 = (0.85 * n((K, H)) / s / np.sqrt(K)).astype(np.float32)
    w4_words, w4_scales = pack_weight(n((H, H)) / u / np.sqrt(H), "e4m3")
    w5 = (n((H, N)) / u / np.sqrt(H)).astype(np.float32)
    perm = np.random.permutation(S)
    return {"tab_words": tab_words, "tab_scales": tab_scales,
            "offs": striped(np.random.permutation(T)[:S]),
            "pos1": striped(perm[:P]), "pos2": striped(perm[P:]),
            "w1": w1, "w2_words": w2_words, "w2_scales": w2_scales, "w3": w3,
            "thr": n(H).astype(np.float32),
            "mat": (2.5 * n((H, P))).astype(np.float32),
            "lift": (0.7 * n(H)).astype(np.float32),
            "wgs": np.exp(0.3 * n((128, P))).astype(np.float32),
            "gain": (np.random.uniform(0.6, 1.6, H) * u[:, 0]).astype(np.float32),
            "w4_words": w4_words, "w4_scales": w4_scales,
            "gain2": (np.random.uniform(0.6, 1.6, H) * u[:, 0]).astype(np.float32),
            "w5": w5}

def reference(tab_words, tab_scales, offs, pos1, pos2, w1, w2_words, w2_scales, w3, thr, mat, lift, wgs, gain, w4_words, w4_scales, gain2, w5):
    v = unpack_weight(tab_words, tab_scales, "e4m3")[:, unstriped(offs)]
    w2 = unpack_weight(w2_words, w2_scales, "e2m1")
    w4 = unpack_weight(w4_words, w4_scales, "e4m3")
    left = mxq(f64(w1), 0, "e4m3").T @ v
    right = w2.T @ v
    ground = mxq(f64(w3), 0, "e4m3").T @ v
    h = np.maximum(left, right) * ground
    a = 1.0 / (1.0 + np.exp(-(h[:, unstriped(pos1)] + f64(thr)[:, None])))
    a = a * f64(mat)
    page = h + f64(lift)[:, None]
    page[:, unstriped(pos2)] = np.tile(f64(wgs), (H // 128, 1)) * a
    page = f64(gain)[:, None] * page
    b = (w4.T @ mxq(page, 0, "e4m3")) + h
    b = f64(gain2)[:, None] * b
    return mxq(f64(w5), 0, "e4m3").T @ mxq(b, 0, "e4m3")

@@ -1,0 +1,359 @@
+from contextlib import ExitStack
+
+import concourse.mybir as mybir
+
+K, T, S, NP, H, N = 1024, 4096, 1024, 512, 512, 768
+FLOPS = 2 * (3 * K * H * S + H * H * S + H * N * S)
+
+F32 = mybir.dt.float32
+BF16 = mybir.dt.bfloat16
+I32 = mybir.dt.int32
+U32 = mybir.dt.uint32
+U16 = mybir.dt.uint16
+U8 = mybir.dt.uint8
+E4M3 = mybir.dt.float8_e4m3fn_x4
+E2M1 = mybir.dt.float4_e2m1fn_x4
+ALU = mybir.AluOpType
+ACT = mybir.ActivationFunctionType
+
+P = 128
+PACK = 4
+PASSES = K // (P * PACK)
+HALF = 512
+EDGES = (0, 128, 384, 640, 896, 1024)
+OUT_TILES = N // P
+
+
+def tile_list_pile_loop_readout_kernel(
+    tc, tab_words, tab_scales, offs, pos1, pos2, w1, w2_words, w2_scales, w3, thr, mat, lift, wgs, gain,
+    w4_words, w4_scales, gain2, w5, out,
+):
+    nc = tc.nc
+
+    with ExitStack() as ctx:
+        lists = ctx.enter_context(tc.tile_pool(name="lists", bufs=1))
+        keep = ctx.enter_context(tc.tile_pool(name="keep", bufs=1))
+        psum = ctx.enter_context(tc.psum_pool(name="psum", bufs=8))
+
+        def kept(name, shape, dtype):
+            return keep.tile(shape, dtype, name=name, align_bytes=64)
+
+        def bank(shape):
+            return psum.tile(shape, F32, name="bank")
+
+        offs_sb = lists.tile([P, S // 16], U16, name="offs_sb")
+        pos1_sb = lists.tile([P, NP // 16], U16, name="pos1_sb")
+        pos2_sb = lists.tile([P, NP // 16], U16, name="pos2_sb")
+
+        v_words = [[kept(f"v_words{a}{u}", [P, HALF], U32) for u in range(2)] for a in range(PASSES)]
+        v_scales = [kept(f"v_scales{a}", [P, S], U8) for a in range(PASSES)]
+        w1_codes = [kept(f"w1_codes{a}", [P, H], U32) for a in range(PASSES)]
+        w1_scales = [kept(f"w1_scales{a}", [P, H], U8) for a in range(PASSES)]
+        w3_codes = [kept(f"w3_codes{a}", [P, H], U32) for a in range(PASSES)]
+        w3_scales = [kept(f"w3_scales{a}", [P, H], U8) for a in range(PASSES)]
+        w2_codes = kept("w2_codes", [P, PASSES, 2 * H], U8)
+        w2_plane = kept("w2_plane", [P, PASSES, H], U8)
+        w4_raw = kept("w4_raw", [P, H], I32)
+        w4_plane_raw = kept("w4_plane_raw", [P, H], U8)
+        w4_codes = kept("w4_codes", [P, H], I32)
+        w4_plane = kept("w4_plane", [P, H], U8)
+        w5_raw = kept("w5_raw", [P, PACK, N], F32)
+        w5_bf = kept("w5_bf", [P, N, PACK], BF16)
+        w5_codes = kept("w5_codes", [P, N], U32)
+        w5_plane = kept("w5_plane", [P, N], U8)
+        thr_sb = kept("thr_sb", [P, PACK], F32)
+        lift_sb = kept("lift_sb", [P, PACK], F32)
+        gain_sb = kept("gain_sb", [P, PACK], F32)
+        gain2_sb = kept("gain2_sb", [P, PACK], F32)
+        side = kept("side", [P, PACK, S], F32)
+        h = [kept(f"h{t}", [P, S], F32) for t in range(PACK)]
+        page = [kept(f"page{t}", [P, S], F32) for t in range(PACK)]
+        look = [kept(f"look{t}", [P, NP], F32) for t in range(PACK)]
+        mat_sb = [kept(f"mat{u}", [P, 2, NP], F32) for u in range(2)]
+        wgs_sb = [kept(f"wgs{u}", [P, 2, NP], F32) for u in range(2)]
+
+        def stage1(dst_fn, codes, scales, dtype, t):
+            width = 2 if dtype is E2M1 else 1
+            for u in range(2):
+                acc = bank([P, HALF])
+                for a in range(PASSES):
+                    nc.tensor.matmul_mx(
+                        out=acc[:],
+                        lhsT=codes(a)[:, width * P * t : width * P * (t + 1)].bitcast(dtype),
+                        lhsT_scale=scales(a)[:, P * t : P * (t + 1)],
+                        rhs=v_words[a][u][:].bitcast(E4M3),
+                        rhs_scale=v_scales[a][:, HALF * u : HALF * (u + 1)],
+                        start=(a == 0),
+                        stop=(a == PASSES - 1),
+                    )
+                dst_fn(acc, slice(HALF * u, HALF * (u + 1)))
+
+        with tc.tile_pool(name="early", bufs=1) as early:
+
+            def staged(name, shape, dtype):
+                return early.tile(shape, dtype, name=name, align_bytes=64)
+
+            tab_sb = [staged(f"tab{a}", [P, T], I32) for a in range(PASSES)]
+            tab_plane = staged("tab_plane", [P, PASSES * T], U8)
+            w2_raw = staged("w2_raw", [P, PASSES, 2 * H], U8)
+            w2_plane_raw = staged("w2_plane_raw", [P, PASSES, H], U8)
+            w1_raw = [staged(f"w1_raw{a}", [P, PACK, H], F32) for a in range(PASSES)]
+            w3_raw = [staged(f"w3_raw{a}", [P, PACK, H], F32) for a in range(PASSES)]
+            w1_bf = [staged(f"w1_bf{a}", [P, PACK, P, PACK], BF16) for a in range(PASSES)]
+            w3_bf = [staged(f"w3_bf{a}", [P, PACK, P, PACK], BF16) for a in range(PASSES)]
+
+            nc.vector.memset(tab_plane[:, 0 : 5 * 1024].bitcast(I32), 0)
+            nc.gpsimd.memset(tab_plane[:, 5 * 1024 : PASSES * T].bitcast(I32), 0)
+            nc.vector.memset(w2_plane_raw[:].rearrange("p a c -> p (a c)").bitcast(I32), 0)
+            nc.gpsimd.memset(w4_plane_raw[:].bitcast(I32), 0)
+
+            def load_rows(dst, w, a):
+                rows = w[a * P * PACK : (a + 1) * P * PACK, :]
+                nc.sync.dma_start(out=dst[:], in_=rows.rearrange("(p j) c -> p j c", j=PACK))
+
+            def load_table(a):
+                nc.sync.dma_start(out=tab_sb[a][:], in_=tab_words[a].rearrange("p t i -> p (t i)").bitcast(I32))
+
+            nc.sync.dma_start(offs_sb[:], offs)
+            nc.sync.dma_start(
+                out=w2_raw[:].bitcast(I32), in_=w2_words.rearrange("a p c -> p a c").bitcast(I32)
+            )
+            tab_plane_3d = tab_plane[:].rearrange("p (a t) -> p a t", a=PASSES)
+            for r in range(4):
+                nc.sync.dma_start(
+                    out=tab_plane_3d[r:P:32].bitcast(I32),
+                    in_=tab_scales[:, r:16:4, :].rearrange("a q t -> q a t").bitcast(I32),
+                )
+            load_table(0)
+            load_rows(w1_raw[0], w1, 0)
+            for r in range(4):
+                nc.sync.dma_start(
+                    out=w2_plane_raw[r:P:32].bitcast(I32),
+                    in_=w2_scales[:, r:16:4, :].rearrange("a q c -> q a c").bitcast(I32),
+                )
+            load_table(1)
+            load_rows(w1_raw[1], w1, 1)
+            load_rows(w3_raw[0], w3, 0)
+            load_rows(w3_raw[1], w3, 1)
+            mat_rows = mat.rearrange("(p t) j -> p t j", t=PACK)
+            wgs_rows = wgs.rearrange("(q t) j -> q t j", t=PACK)
+            load_rows(w5_raw, w5, 0)
+            nc.sync.dma_start(pos1_sb[:], pos1)
+            nc.sync.dma_start(pos2_sb[:], pos2)
+            nc.sync.dma_start(out=w4_raw[:], in_=w4_words[0].rearrange("p c i -> p (c i)").bitcast(I32))
+            for r in range(4):
+                nc.sync.dma_start(
+                    out=w4_plane_raw[r:P:32, :].bitcast(I32),
+                    in_=w4_scales[0, r:16:4, :].bitcast(I32),
+                )
+            for u in range(2):
+                nc.sync.dma_start(out=mat_sb[u][:], in_=mat_rows[:, 2 * u : 2 * u + 2, :])
+                for q in range(4):
+                    nc.sync.dma_start(out=wgs_sb[u][32 * q : 32 * q + 32], in_=wgs_rows[:, 2 * u : 2 * u + 2, :])
+
+            for dst, vec in ((thr_sb, thr), (lift_sb, lift), (gain_sb, gain), (gain2_sb, gain2)):
+                nc.gpsimd.dma_start(out=dst[:], in_=vec.rearrange("(p t) -> p t", t=PACK))
+
+            def gather_words(a):
+                for u in range(2):
+                    cols = slice(u * HALF // 16, (u + 1) * HALF // 16)
+                    nc.vector.tensor_copy(
+                        out=v_words[a][u][:], in_=tab_sb[a][:].bitcast(U32).indirect(offs_sb[:, cols])
+                    )
+
+            def deal_views(raw, bf, m0, m1):
+                dst = bf[:].rearrange("p t m j -> p m t j")[:, m0:m1]
+                src = raw[:].rearrange("p j (m t) -> p m t j", t=PACK)[:, m0:m1]
+                return dst, src
+
+            def quantise(bf, codes, scales, t0, t1):
+                nc.vector.quantize_mx(
+                    out=codes[:, P * t0 : P * t1].bitcast(E4M3),
+                    scales=scales[:, P * t0 : P * t1],
+                    in_=bf[:, t0:t1].rearrange("p t m j -> p (t m j)"),
+                )
+
+            nc.vector.tensor_copy(
+                out=w2_codes[:].bitcast(U16).rearrange("p a (t m) -> p a t m", t=PACK),
+                in_=w2_raw[:].bitcast(U16).rearrange("p a (m t) -> p a t m", t=PACK),
+            )
+            for a in range(PASSES):
+                nc.vector.tensor_copy(
+                    out=v_scales[a][:], in_=tab_plane[:, a * T : (a + 1) * T].indirect(offs_sb[:])
+                )
+            gather_words(0)
+            nc.vector.tensor_copy(
+                out=w2_plane[:].rearrange("p a (t m) -> p a t m", t=PACK),
+                in_=w2_plane_raw[:].rearrange("p a (m t) -> p a t m", t=PACK),
+            )
+            gather_words(1)
+            dst, src = deal_views(w1_raw[0], w1_bf[0], 0, P)
+            nc.scalar.copy(out=dst, in_=src)
+            dst, src = deal_views(w1_raw[1], w1_bf[1], 0, P)
+            nc.vector.tensor_copy(out=dst, in_=src)
+            for a in range(PASSES):
+                quantise(w1_bf[a], w1_codes[a], w1_scales[a], 0, PACK)
+
+            for t in range(PACK):
+                stage1(
+                    lambda acc, cols, t=t: nc.scalar.copy(out=side[:, t, cols], in_=acc[:]),
+                    lambda a: w2_codes[:, a, :], lambda a: w2_plane[:, a, :], E2M1, t,
+                )
+
+            def larger(t):
+                stage1(
+                    lambda acc, cols: nc.vector.tensor_tensor(
+                        out=side[:, t, cols], in0=acc[:], in1=side[:, t, cols], op=ALU.max
+                    ),
+                    lambda a: w1_codes[a], lambda a: w1_scales[a], E4M3, t,
+                )
+
+            for a in range(PASSES):
+                dst, src = deal_views(w3_raw[a], w3_bf[a], 0, P)
+                nc.scalar.copy(out=dst, in_=src)
+                quantise(w3_bf[a], w3_codes[a], w3_scales[a], 0, PACK)
+            for t in range(PACK):
+                larger(t)
+
+        def features(t):
+            stage1(
+                lambda acc, cols: nc.vector.tensor_tensor(
+                    out=h[t][:, cols], in0=acc[:], in1=side[:, t, cols], op=ALU.mult
+                ),
+                lambda a: w3_codes[a], lambda a: w3_scales[a], E4M3, t,
+            )
+
+        def fetch(t):
+            nc.scalar.activation(
+                out=look[t][:], in_=h[t][:].indirect(pos1_sb[:]), func=ACT.Sigmoid, bias=thr_sb[:, t : t + 1]
+            )
+
+        def fill(t):
+            nc.scalar.activation(out=page[t][:], in_=h[t][:], func=ACT.Identity, bias=lift_sb[:, t : t + 1])
+
+        def put(t):
+            u, e = divmod(t, 2)
+            nc.gpsimd.tensor_tensor(out=mat_sb[u][:, e, :], in0=mat_sb[u][:, e, :], in1=wgs_sb[u][:, e, :], op=ALU.mult)
+            nc.vector.tensor_tensor(
+                out=page[t][:].indirect(pos2_sb[:]), in0=look[t][:], in1=mat_sb[u][:, e, :], op=ALU.mult
+            )
+
+        for t in range(PACK):
+            features(t)
+        nc.scalar.copy(
+            out=w5_bf[:].rearrange("p (c i) j -> p c j i", i=4),
+            in_=w5_raw[:].rearrange("p j (c i) -> p c j i", i=4),
+        )
+        for t in range(PACK):
+            fetch(t)
+            fill(t)
+
+        nc.vector.tensor_copy(
+            out=w4_plane[:].rearrange("p (t m) -> p t m", t=PACK),
+            in_=w4_plane_raw[:].rearrange("p (m t) -> p t m", t=PACK),
+        )
+        nc.vector.tensor_copy(
+            out=w4_codes[:].rearrange("p (t m) -> p t m", t=PACK), in_=w4_raw[:].rearrange("p (m t) -> p t m", t=PACK)
+        )
+        for half in range(2):
+            cols = slice(half * N // 2, (half + 1) * N // 2)
+            nc.vector.quantize_mx(
+                out=w5_codes[:, cols].bitcast(E4M3),
+                scales=w5_plane[:, cols],
+                in_=w5_bf[:, cols, :].rearrange("p c j -> p (c j)"),
+            )
+
+        for t in range(PACK):
+            nc.gpsimd.tensor_scalar(
+                out=side[:, t, :], in0=h[t][:], scalar1=gain2_sb[:, t : t + 1], scalar2=0.0, op0=ALU.mult, op1=ALU.add
+            )
+        for t in range(PACK):
+            put(t)
+
+        late = ctx.enter_context(tc.tile_pool(name="late", bufs=5))
+        page_bf = late.tile([P, PACK, S], BF16, name="page_bf", bufs=1, align_bytes=64)
+
+        def round_page(t, cols):
+            nc.scalar.activation(out=page_bf[:, t, cols], in_=page[t][:, cols], func=ACT.Copy, scale=gain_sb[:, t : t + 1])
+
+        for t in range(PACK - 1):
+            round_page(t, slice(0, S))
+
+        out_rows = out.rearrange("(i p) j -> p i j", p=P)
+        chunks = len(EDGES) - 1
+        state = {}
+
+        def step_a(c):
+            cols = slice(EDGES[c], EDGES[c + 1])
+            width = EDGES[c + 1] - EDGES[c]
+            round_page(PACK - 1, cols)
+            a_bf = late.tile([P, width, PACK], BF16, name="a_bf", align_bytes=64)
+            nc.vector.tensor_copy(
+                out=a_bf[:].rearrange("p (c i) t -> p c t i", i=4),
+                in_=page_bf[:, :, cols].rearrange("p t (c i) -> p c t i", i=4),
+            )
+            a_codes = late.tile([P, width], U32, name="a_codes", align_bytes=64)
+            a_plane = late.tile([P, width], U8, name="a_plane", align_bytes=64)
+            nc.vector.quantize_mx(
+                out=a_codes[:].bitcast(E4M3), scales=a_plane[:], in_=a_bf[:].rearrange("p c t -> p (c t)")
+            )
+            y = late.tile([P, PACK, width], F32, name="y", align_bytes=64)
+            for pair in range(2):
+                acc = bank([P, 2, width])
+                for e in range(2):
+                    t = 2 * pair + e
+                    nc.tensor.matmul_mx(
+                        out=acc[:, e, :],
+                        lhsT=w4_codes[:, P * t : P * (t + 1)].bitcast(E4M3),
+                        lhsT_scale=w4_plane[:, P * t : P * (t + 1)],
+                        rhs=a_codes[:].bitcast(E4M3),
+                        rhs_scale=a_plane[:],
+                        start=True,
+                        stop=True,
+                    )
+                for e in range(2):
+                    t = 2 * pair + e
+                    nc.scalar.activation(out=y[:, t, :], in_=acc[:, e, :], func=ACT.Copy, scale=gain2_sb[:, t : t + 1])
+            state[c] = y
+
+        def step_b(c):
+            cols = slice(EDGES[c], EDGES[c + 1])
+            width = EDGES[c + 1] - EDGES[c]
+            y = state[c]
+            b_bf = late.tile([P, width, PACK], BF16, name="b_bf", align_bytes=64)
+            nc.vector.tensor_tensor(
+                out=b_bf[:].rearrange("p (c i) t -> p c t i", i=2),
+                in0=y[:].rearrange("p t (c i) -> p c t i", i=2),
+                in1=side[:, :, cols].rearrange("p t (c i) -> p c t i", i=2),
+                op=ALU.add,
+            )
+            b_codes = late.tile([P, width], U32, name="b_codes", align_bytes=64)
+            b_plane = late.tile([P, width], U8, name="b_plane", align_bytes=64)
+            nc.vector.quantize_mx(
+                out=b_codes[:].bitcast(E4M3), scales=b_plane[:], in_=b_bf[:].rearrange("p c t -> p (c t)")
+            )
+            for pair in range(OUT_TILES // 2):
+                acc = bank([P, 2, width])
+                for e in range(2):
+                    i = 2 * pair + e
+                    nc.tensor.matmul_mx(
+                        out=acc[:, e, :],
+                        lhsT=w5_codes[:, P * i : P * (i + 1)].bitcast(E4M3),
+                        lhsT_scale=w5_plane[:, P * i : P * (i + 1)],
+                        rhs=b_codes[:].bitcast(E4M3),
+                        rhs_scale=b_plane[:],
+                        start=True,
+                        stop=True,
+                    )
+                res = late.tile([P, 2, width], F32, name="res", bufs=6, align_bytes=64)
+                if pair == 1 and c > 0:
+                    nc.vector.tensor_copy(out=res[:], in_=acc[:])
+                else:
+                    nc.scalar.copy(out=res[:], in_=acc[:])
+                nc.sync.dma_start(out=out_rows[:, 2 * pair : 2 * pair + 2, cols], in_=res[:])
+
+        step_a(0)
+        for c in range(chunks):
+            if c + 1 < chunks:
+                step_a(c + 1)
+            step_b(c)

@@ -57,7 +57,7 @@ def tile_list_pile_loop_readout_kernel(
         w4_plane_raw = kept("w4_plane_raw", [P, H], U8)
         w4_codes = kept("w4_codes", [P, H], I32)
         w4_plane = kept("w4_plane", [P, H], U8)
-        w5_raw = kept("w5_raw", [P, PACK, N], F32)
+        w5_raw = keep.tile([P, PACK, N], F32, name="w5_raw", tag="w5_then_page_bf", align_bytes=64)
         w5_bf = kept("w5_bf", [P, N, PACK], BF16)
         w5_codes = kept("w5_codes", [P, N], U32)
         w5_plane = kept("w5_plane", [P, N], U8)
@@ -70,7 +70,7 @@ def tile_list_pile_loop_readout_kernel(
         page = [kept(f"page{t}", [P, S], F32) for t in range(PACK)]
         look = [kept(f"look{t}", [P, NP], F32) for t in range(PACK)]
         mat_sb = [kept(f"mat{u}", [P, 2, NP], F32) for u in range(2)]
-        wgs_sb = [kept(f"wgs{u}", [P, 2, NP], F32) for u in range(2)]
+        wgs_sb = keep.tile([P, PACK, NP], F32, name="wgs_sb", tag="wgs_then_skip", align_bytes=64)
 
         def stage1(dst_fn, codes, scales, dtype, t):
             width = 2 if dtype is E2M1 else 1
@@ -137,7 +137,6 @@ def tile_list_pile_loop_readout_kernel(
             load_rows(w3_raw[1], w3, 1)
             mat_rows = mat.rearrange("(p t) j -> p t j", t=PACK)
             wgs_rows = wgs.rearrange("(q t) j -> q t j", t=PACK)
-            load_rows(w5_raw, w5, 0)
             nc.sync.dma_start(pos1_sb[:], pos1)
             nc.sync.dma_start(pos2_sb[:], pos2)
             nc.sync.dma_start(out=w4_raw[:], in_=w4_words[0].rearrange("p c i -> p (c i)").bitcast(I32))
@@ -148,8 +147,11 @@ def tile_list_pile_loop_readout_kernel(
                 )
             for u in range(2):
                 nc.sync.dma_start(out=mat_sb[u][:], in_=mat_rows[:, 2 * u : 2 * u + 2, :])
-                for q in range(4):
-                    nc.sync.dma_start(out=wgs_sb[u][32 * q : 32 * q + 32], in_=wgs_rows[:, 2 * u : 2 * u + 2, :])
+                for q in (0, 2, 1, 3):
+                    nc.sync.dma_start(
+                        out=wgs_sb[32 * q : 32 * q + 32, 2 * u : 2 * u + 2, :], in_=wgs_rows[:, 2 * u : 2 * u + 2, :]
+                    )
+            load_rows(w5_raw, w5, 0)
 
             for dst, vec in ((thr_sb, thr), (lift_sb, lift), (gain_sb, gain), (gain2_sb, gain2)):
                 nc.gpsimd.dma_start(out=dst[:], in_=vec.rearrange("(p t) -> p t", t=PACK))
@@ -212,8 +214,7 @@ def tile_list_pile_loop_readout_kernel(
                 dst, src = deal_views(w3_raw[a], w3_bf[a], 0, P)
                 nc.scalar.copy(out=dst, in_=src)
                 quantise(w3_bf[a], w3_codes[a], w3_scales[a], 0, PACK)
-            for t in range(PACK):
-                larger(t)
+            larger(0)
 
         def features(t):
             stage1(
@@ -233,51 +234,50 @@ def tile_list_pile_loop_readout_kernel(
 
         def put(t):
             u, e = divmod(t, 2)
-            nc.gpsimd.tensor_tensor(out=mat_sb[u][:, e, :], in0=mat_sb[u][:, e, :], in1=wgs_sb[u][:, e, :], op=ALU.mult)
+            nc.gpsimd.tensor_tensor(out=mat_sb[u][:, e, :], in0=mat_sb[u][:, e, :], in1=wgs_sb[:, t, :], op=ALU.mult)
             nc.vector.tensor_tensor(
                 out=page[t][:].indirect(pos2_sb[:]), in0=look[t][:], in1=mat_sb[u][:, e, :], op=ALU.mult
             )
 
         for t in range(PACK):
+            if t + 1 < PACK:
+                larger(t + 1)
             features(t)
+        for t in range(PACK):
+            fetch(t)
+            fill(t)
         nc.scalar.copy(
             out=w5_bf[:].rearrange("p (c i) j -> p c j i", i=4),
             in_=w5_raw[:].rearrange("p j (c i) -> p c j i", i=4),
         )
-        for t in range(PACK):
-            fetch(t)
-            fill(t)
 
-        nc.vector.tensor_copy(
+        nc.gpsimd.tensor_copy(
             out=w4_plane[:].rearrange("p (t m) -> p t m", t=PACK),
             in_=w4_plane_raw[:].rearrange("p (m t) -> p t m", t=PACK),
         )
-        nc.vector.tensor_copy(
+        nc.gpsimd.tensor_copy(
             out=w4_codes[:].rearrange("p (t m) -> p t m", t=PACK), in_=w4_raw[:].rearrange("p (m t) -> p t m", t=PACK)
         )
-        for half in range(2):
-            cols = slice(half * N // 2, (half + 1) * N // 2)
-            nc.vector.quantize_mx(
-                out=w5_codes[:, cols].bitcast(E4M3),
-                scales=w5_plane[:, cols],
-                in_=w5_bf[:, cols, :].rearrange("p c j -> p (c j)"),
-            )
-
-        for t in range(PACK):
-            nc.gpsimd.tensor_scalar(
-                out=side[:, t, :], in0=h[t][:], scalar1=gain2_sb[:, t : t + 1], scalar2=0.0, op0=ALU.mult, op1=ALU.add
-            )
         for t in range(PACK):
             put(t)
 
         late = ctx.enter_context(tc.tile_pool(name="late", bufs=5))
-        page_bf = late.tile([P, PACK, S], BF16, name="page_bf", bufs=1, align_bytes=64)
+        page_bf = keep.tile([P, PACK, S], BF16, name="page_bf", tag="w5_then_page_bf", align_bytes=64)
 
         def round_page(t, cols):
             nc.scalar.activation(out=page_bf[:, t, cols], in_=page[t][:, cols], func=ACT.Copy, scale=gain_sb[:, t : t + 1])
 
         for t in range(PACK - 1):
             round_page(t, slice(0, S))
+        skip = keep.tile([P, PACK, S], F32, name="skip", tag="wgs_then_skip", align_bytes=64)
+        for t in range(PACK):
+            if t < 2:
+                nc.gpsimd.tensor_scalar(
+                    out=skip[:, t, :], in0=h[t][:], scalar1=gain2_sb[:, t : t + 1], scalar2=0.0,
+                    op0=ALU.mult, op1=ALU.add,
+                )
+            else:
+                nc.scalar.activation(out=skip[:, t, :], in_=h[t][:], func=ACT.Copy, scale=gain2_sb[:, t : t + 1])
 
         out_rows = out.rearrange("(i p) j -> p i j", p=P)
         chunks = len(EDGES) - 1
@@ -324,7 +324,7 @@ def tile_list_pile_loop_readout_kernel(
             nc.vector.tensor_tensor(
                 out=b_bf[:].rearrange("p (c i) t -> p c t i", i=2),
                 in0=y[:].rearrange("p t (c i) -> p c t i", i=2),
-                in1=side[:, :, cols].rearrange("p t (c i) -> p c t i", i=2),
+                in1=skip[:, :, cols].rearrange("p t (c i) -> p c t i", i=2),
                 op=ALU.add,
             )
             b_codes = late.tile([P, width], U32, name="b_codes", align_bytes=64)
@@ -353,6 +353,14 @@ def tile_list_pile_loop_readout_kernel(
                 nc.sync.dma_start(out=out_rows[:, 2 * pair : 2 * pair + 2, cols], in_=res[:])
 
         step_a(0)
+        for half in range(2):
+            cols = slice(half * N // 2, (half + 1) * N // 2)
+            nc.vector.quantize_mx(
+                out=w5_codes[:, cols].bitcast(E4M3),
+                scales=w5_plane[:, cols],
+                in_=w5_bf[:, cols, :].rearrange("p c j -> p (c j)"),
+            )
+
         for c in range(chunks):
             if c + 1 < chunks:
                 step_a(c + 1)

@@ -94,7 +94,8 @@ def tile_list_pile_loop_readout_kernel(
                 return early.tile(shape, dtype, name=name, align_bytes=64)
 
             tab_sb = [staged(f"tab{a}", [P, T], I32) for a in range(PASSES)]
-            tab_plane = staged("tab_plane", [P, PASSES * T], U8)
+            tab_plane = staged("tab_plane", [P, T], U8)
+            picked_rows = staged("picked_rows", [P, S], U8)
             w2_raw = staged("w2_raw", [P, PASSES, 2 * H], U8)
             w2_plane_raw = staged("w2_plane_raw", [P, PASSES, H], U8)
             w1_raw = [staged(f"w1_raw{a}", [P, PACK, H], F32) for a in range(PASSES)]
@@ -102,8 +103,9 @@ def tile_list_pile_loop_readout_kernel(
             w1_bf = [staged(f"w1_bf{a}", [P, PACK, P, PACK], BF16) for a in range(PASSES)]
             w3_bf = [staged(f"w3_bf{a}", [P, PACK, P, PACK], BF16) for a in range(PASSES)]
 
-            nc.vector.memset(tab_plane[:, 0 : 5 * 1024].bitcast(I32), 0)
-            nc.gpsimd.memset(tab_plane[:, 5 * 1024 : PASSES * T].bitcast(I32), 0)
+            nc.vector.memset(tab_plane[0:96].bitcast(I32), 0)
+            for a in range(PASSES):
+                nc.vector.memset(v_scales[a][:].bitcast(I32), 0)
             nc.vector.memset(w2_plane_raw[:].rearrange("p a c -> p (a c)").bitcast(I32), 0)
             nc.gpsimd.memset(w4_plane_raw[:].bitcast(I32), 0)
 
@@ -116,14 +118,11 @@ def tile_list_pile_loop_readout_kernel(
 
             nc.sync.dma_start(offs_sb[:], offs)
             nc.sync.dma_start(
+                out=tab_plane[96:P].bitcast(I32), in_=tab_scales.rearrange("a q t -> (a q) t").bitcast(I32)
+            )
+            nc.sync.dma_start(
                 out=w2_raw[:].bitcast(I32), in_=w2_words.rearrange("a p c -> p a c").bitcast(I32)
             )
-            tab_plane_3d = tab_plane[:].rearrange("p (a t) -> p a t", a=PASSES)
-            for r in range(4):
-                nc.sync.dma_start(
-                    out=tab_plane_3d[r:P:32].bitcast(I32),
-                    in_=tab_scales[:, r:16:4, :].rearrange("a q t -> q a t").bitcast(I32),
-                )
             load_table(0)
             load_rows(w1_raw[0], w1, 0)
             for r in range(4):
@@ -153,8 +152,6 @@ def tile_list_pile_loop_readout_kernel(
                     )
             load_rows(w5_raw, w5, 0)
 
-            for dst, vec in ((thr_sb, thr), (lift_sb, lift), (gain_sb, gain), (gain2_sb, gain2)):
-                nc.gpsimd.dma_start(out=dst[:], in_=vec.rearrange("(p t) -> p t", t=PACK))
 
             def gather_words(a):
                 for u in range(2):
@@ -179,10 +176,15 @@ def tile_list_pile_loop_readout_kernel(
                 out=w2_codes[:].bitcast(U16).rearrange("p a (t m) -> p a t m", t=PACK),
                 in_=w2_raw[:].bitcast(U16).rearrange("p a (m t) -> p a t m", t=PACK),
             )
+            nc.vector.tensor_copy(out=picked_rows[:], in_=tab_plane[:].indirect(offs_sb[:]))
             for a in range(PASSES):
-                nc.vector.tensor_copy(
-                    out=v_scales[a][:], in_=tab_plane[:, a * T : (a + 1) * T].indirect(offs_sb[:])
-                )
+                for q in range(4):
+                    first = 96 + 16 * a + 4 * q
+                    nc.gpsimd.dma_start(
+                        out=v_scales[a][32 * q : 32 * q + 4].bitcast(I32), in_=picked_rows[first : first + 4].bitcast(I32)
+                    )
+            for dst, vec in ((thr_sb, thr), (lift_sb, lift), (gain_sb, gain), (gain2_sb, gain2)):
+                nc.gpsimd.dma_start(out=dst[:], in_=vec.rearrange("(p t) -> p t", t=PACK))
             gather_words(0)
             nc.vector.tensor_copy(
                 out=w2_plane[:].rearrange("p a (t m) -> p a t m", t=PACK),

@@ -56,10 +56,8 @@ def tile_list_pile_loop_readout_kernel(
         w4_raw = kept("w4_raw", [P, H], I32)
         w4_plane_raw = kept("w4_plane_raw", [P, H], U8)
         w4_codes = kept("w4_codes", [P, H], I32)
-        w4_plane = kept("w4_plane", [P, H], U8)
         w5_raw = keep.tile([P, PACK, N], F32, name="w5_raw", tag="w5_then_page_bf", align_bytes=64)
         w5_bf = kept("w5_bf", [P, N, PACK], BF16)
-        w5_codes = kept("w5_codes", [P, N], U32)
         w5_plane = kept("w5_plane", [P, N], U8)
         thr_sb = kept("thr_sb", [P, PACK], F32)
         lift_sb = kept("lift_sb", [P, PACK], F32)
@@ -68,9 +66,14 @@ def tile_list_pile_loop_readout_kernel(
         side = kept("side", [P, PACK, S], F32)
         h = [kept(f"h{t}", [P, S], F32) for t in range(PACK)]
         page = [kept(f"page{t}", [P, S], F32) for t in range(PACK)]
-        look = [kept(f"look{t}", [P, NP], F32) for t in range(PACK)]
+        look = [kept(f"look{t}", [P, NP], F32) for t in range(PACK - 1)]
+        look.append(keep.tile([P, NP], F32, name="look3", tag="look_then_w5_codes", align_bytes=64))
         mat_sb = [kept(f"mat{u}", [P, 2, NP], F32) for u in range(2)]
-        wgs_sb = keep.tile([P, PACK, NP], F32, name="wgs_sb", tag="wgs_then_skip", align_bytes=64)
+        wgs_sb = [
+            keep.tile([P, 2, NP], F32, name="wgs0", tag="wgs_then_skip", align_bytes=64),
+            kept("wgs1", [P, 2, NP], F32),
+        ]
+        w1_bf_first = keep.tile([P, PACK, P, PACK], BF16, name="w1_bf0", tag="w1_bf_then_w4_plane", align_bytes=64)
 
         def stage1(dst_fn, codes, scales, dtype, t):
             width = 2 if dtype is E2M1 else 1
@@ -100,13 +103,13 @@ def tile_list_pile_loop_readout_kernel(
             w2_plane_raw = staged("w2_plane_raw", [P, PASSES, H], U8)
             w1_raw = [staged(f"w1_raw{a}", [P, PACK, H], F32) for a in range(PASSES)]
             w3_raw = [staged(f"w3_raw{a}", [P, PACK, H], F32) for a in range(PASSES)]
-            w1_bf = [staged(f"w1_bf{a}", [P, PACK, P, PACK], BF16) for a in range(PASSES)]
+            w1_bf = [w1_bf_first, staged("w1_bf1", [P, PACK, P, PACK], BF16)]
             w3_bf = [staged(f"w3_bf{a}", [P, PACK, P, PACK], BF16) for a in range(PASSES)]
 
             nc.vector.memset(tab_plane[0:96].bitcast(I32), 0)
             for a in range(PASSES):
                 nc.vector.memset(v_scales[a][:].bitcast(I32), 0)
-            nc.vector.memset(w2_plane_raw[:].rearrange("p a c -> p (a c)").bitcast(I32), 0)
+            nc.gpsimd.memset(w2_plane_raw[:].rearrange("p a c -> p (a c)").bitcast(I32), 0)
             nc.gpsimd.memset(w4_plane_raw[:].bitcast(I32), 0)
 
             def load_rows(dst, w, a):
@@ -124,13 +127,30 @@ def tile_list_pile_loop_readout_kernel(
                 out=w2_raw[:].bitcast(I32), in_=w2_words.rearrange("a p c -> p a c").bitcast(I32)
             )
             load_table(0)
-            load_rows(w1_raw[0], w1, 0)
+            load_table(1)
+
             for r in range(4):
-                nc.sync.dma_start(
+                nc.gpsimd.dma_start(
                     out=w2_plane_raw[r:P:32].bitcast(I32),
                     in_=w2_scales[:, r:16:4, :].rearrange("a q c -> q a c").bitcast(I32),
                 )
-            load_table(1)
+            for r in range(4):
+                nc.gpsimd.dma_start(
+                    out=w4_plane_raw[r:P:32, :].bitcast(I32),
+                    in_=w4_scales[0, r:16:4, :].bitcast(I32),
+                )
+            for dst, vec in ((thr_sb, thr), (lift_sb, lift), (gain_sb, gain), (gain2_sb, gain2)):
+                nc.gpsimd.dma_start(out=dst[:], in_=vec.rearrange("(p t) -> p t", t=PACK))
+
+            nc.vector.tensor_copy(out=picked_rows[:], in_=tab_plane[:].indirect(offs_sb[:]))
+            for a in range(PASSES):
+                for q in range(4):
+                    first = 96 + 16 * a + 4 * q
+                    nc.scalar.dma_start(
+                        out=v_scales[a][32 * q : 32 * q + 4].bitcast(I32), in_=picked_rows[first : first + 4].bitcast(I32)
+                    )
+
+            load_rows(w1_raw[0], w1, 0)
             load_rows(w1_raw[1], w1, 1)
             load_rows(w3_raw[0], w3, 0)
             load_rows(w3_raw[1], w3, 1)
@@ -139,19 +159,15 @@ def tile_list_pile_loop_readout_kernel(
             nc.sync.dma_start(pos1_sb[:], pos1)
             nc.sync.dma_start(pos2_sb[:], pos2)
             nc.sync.dma_start(out=w4_raw[:], in_=w4_words[0].rearrange("p c i -> p (c i)").bitcast(I32))
-            for r in range(4):
-                nc.sync.dma_start(
-                    out=w4_plane_raw[r:P:32, :].bitcast(I32),
-                    in_=w4_scales[0, r:16:4, :].bitcast(I32),
-                )
-            for u in range(2):
-                nc.sync.dma_start(out=mat_sb[u][:], in_=mat_rows[:, 2 * u : 2 * u + 2, :])
-                for q in (0, 2, 1, 3):
-                    nc.sync.dma_start(
-                        out=wgs_sb[32 * q : 32 * q + 32, 2 * u : 2 * u + 2, :], in_=wgs_rows[:, 2 * u : 2 * u + 2, :]
-                    )
-            load_rows(w5_raw, w5, 0)
 
+            def load_factors(u):
+                for q in (0, 2, 1, 3):
+                    nc.sync.dma_start(out=wgs_sb[u][32 * q : 32 * q + 32], in_=wgs_rows[:, 2 * u : 2 * u + 2, :])
+                nc.sync.dma_start(out=mat_sb[u][:], in_=mat_rows[:, 2 * u : 2 * u + 2, :])
+
+            load_factors(0)
+            load_rows(w5_raw, w5, 0)
+            load_factors(1)
 
             def gather_words(a):
                 for u in range(2):
@@ -176,27 +192,21 @@ def tile_list_pile_loop_readout_kernel(
                 out=w2_codes[:].bitcast(U16).rearrange("p a (t m) -> p a t m", t=PACK),
                 in_=w2_raw[:].bitcast(U16).rearrange("p a (m t) -> p a t m", t=PACK),
             )
-            nc.vector.tensor_copy(out=picked_rows[:], in_=tab_plane[:].indirect(offs_sb[:]))
-            for a in range(PASSES):
-                for q in range(4):
-                    first = 96 + 16 * a + 4 * q
-                    nc.gpsimd.dma_start(
-                        out=v_scales[a][32 * q : 32 * q + 4].bitcast(I32), in_=picked_rows[first : first + 4].bitcast(I32)
-                    )
-            for dst, vec in ((thr_sb, thr), (lift_sb, lift), (gain_sb, gain), (gain2_sb, gain2)):
-                nc.gpsimd.dma_start(out=dst[:], in_=vec.rearrange("(p t) -> p t", t=PACK))
-            gather_words(0)
             nc.vector.tensor_copy(
                 out=w2_plane[:].rearrange("p a (t m) -> p a t m", t=PACK),
                 in_=w2_plane_raw[:].rearrange("p a (m t) -> p a t m", t=PACK),
             )
-            gather_words(1)
-            dst, src = deal_views(w1_raw[0], w1_bf[0], 0, P)
-            nc.scalar.copy(out=dst, in_=src)
-            dst, src = deal_views(w1_raw[1], w1_bf[1], 0, P)
-            nc.vector.tensor_copy(out=dst, in_=src)
             for a in range(PASSES):
+                gather_words(a)
+            for a in range(PASSES):
+                dst, src = deal_views(w1_raw[a], w1_bf[a], 0, P)
+                nc.vector.tensor_copy(out=dst, in_=src)
                 quantise(w1_bf[a], w1_codes[a], w1_scales[a], 0, PACK)
+            w4_plane = keep.tile([P, H], U8, name="w4_plane", tag="w1_bf_then_w4_plane", align_bytes=64)
+            nc.vector.tensor_copy(
+                out=w4_plane[:].rearrange("p (t m) -> p t m", t=PACK),
+                in_=w4_plane_raw[:].rearrange("p (m t) -> p t m", t=PACK),
+            )
 
             for t in range(PACK):
                 stage1(
@@ -212,11 +222,20 @@ def tile_list_pile_loop_readout_kernel(
                     lambda a: w1_codes[a], lambda a: w1_scales[a], E4M3, t,
                 )
 
+            dst, src = deal_views(w3_raw[0], w3_bf[0], 0, P)
+            nc.scalar.copy(out=dst, in_=src)
+            dst, src = deal_views(w3_raw[1], w3_bf[1], 0, P // 2)
+            nc.scalar.copy(out=dst, in_=src)
+            dst, src = deal_views(w3_raw[1], w3_bf[1], P // 2, P)
+            nc.vector.tensor_copy(out=dst, in_=src)
             for a in range(PASSES):
-                dst, src = deal_views(w3_raw[a], w3_bf[a], 0, P)
-                nc.scalar.copy(out=dst, in_=src)
                 quantise(w3_bf[a], w3_codes[a], w3_scales[a], 0, PACK)
-            larger(0)
+            for t in range(PACK):
+                larger(t)
+        nc.scalar.copy(
+            out=w4_codes[:].bitcast(U32).rearrange("p (t m) -> p m t", t=PACK),
+            in_=w4_raw[:].bitcast(U32).rearrange("p (m t) -> p m t", t=PACK),
+        )
 
         def features(t):
             stage1(
@@ -236,14 +255,13 @@ def tile_list_pile_loop_readout_kernel(
 
         def put(t):
             u, e = divmod(t, 2)
-            nc.gpsimd.tensor_tensor(out=mat_sb[u][:, e, :], in0=mat_sb[u][:, e, :], in1=wgs_sb[:, t, :], op=ALU.mult)
+            engine = nc.gpsimd if u == 0 else nc.vector
+            engine.tensor_tensor(out=mat_sb[u][:, e, :], in0=mat_sb[u][:, e, :], in1=wgs_sb[u][:, e, :], op=ALU.mult)
             nc.vector.tensor_tensor(
                 out=page[t][:].indirect(pos2_sb[:]), in0=look[t][:], in1=mat_sb[u][:, e, :], op=ALU.mult
             )
 
         for t in range(PACK):
-            if t + 1 < PACK:
-                larger(t + 1)
             features(t)
         for t in range(PACK):
             fetch(t)
@@ -253,13 +271,6 @@ def tile_list_pile_loop_readout_kernel(
             in_=w5_raw[:].rearrange("p j (c i) -> p c j i", i=4),
         )
 
-        nc.gpsimd.tensor_copy(
-            out=w4_plane[:].rearrange("p (t m) -> p t m", t=PACK),
-            in_=w4_plane_raw[:].rearrange("p (m t) -> p t m", t=PACK),
-        )
-        nc.gpsimd.tensor_copy(
-            out=w4_codes[:].rearrange("p (t m) -> p t m", t=PACK), in_=w4_raw[:].rearrange("p (m t) -> p t m", t=PACK)
-        )
         for t in range(PACK):
             put(t)
 
@@ -285,7 +296,7 @@ def tile_list_pile_loop_readout_kernel(
         chunks = len(EDGES) - 1
         state = {}
 
-        def step_a(c):
+        def weave(c):
             cols = slice(EDGES[c], EDGES[c + 1])
             width = EDGES[c + 1] - EDGES[c]
             round_page(PACK - 1, cols)
@@ -294,6 +305,11 @@ def tile_list_pile_loop_readout_kernel(
                 out=a_bf[:].rearrange("p (c i) t -> p c t i", i=4),
                 in_=page_bf[:, :, cols].rearrange("p t (c i) -> p c t i", i=4),
             )
+            state["a", c] = a_bf
+
+        def second_stage(c):
+            width = EDGES[c + 1] - EDGES[c]
+            a_bf = state["a", c]
             a_codes = late.tile([P, width], U32, name="a_codes", align_bytes=64)
             a_plane = late.tile([P, width], U8, name="a_plane", align_bytes=64)
             nc.vector.quantize_mx(
@@ -316,12 +332,12 @@ def tile_list_pile_loop_readout_kernel(
                 for e in range(2):
                     t = 2 * pair + e
                     nc.scalar.activation(out=y[:, t, :], in_=acc[:, e, :], func=ACT.Copy, scale=gain2_sb[:, t : t + 1])
-            state[c] = y
+            state["y", c] = y
 
-        def step_b(c):
+        def join(c):
             cols = slice(EDGES[c], EDGES[c + 1])
             width = EDGES[c + 1] - EDGES[c]
-            y = state[c]
+            y = state["y", c]
             b_bf = late.tile([P, width, PACK], BF16, name="b_bf", align_bytes=64)
             nc.vector.tensor_tensor(
                 out=b_bf[:].rearrange("p (c i) t -> p c t i", i=2),
@@ -329,6 +345,12 @@ def tile_list_pile_loop_readout_kernel(
                 in1=skip[:, :, cols].rearrange("p t (c i) -> p c t i", i=2),
                 op=ALU.add,
             )
+            state["b", c] = b_bf
+
+        def third_stage(c):
+            cols = slice(EDGES[c], EDGES[c + 1])
+            width = EDGES[c + 1] - EDGES[c]
+            b_bf = state["b", c]
             b_codes = late.tile([P, width], U32, name="b_codes", align_bytes=64)
             b_plane = late.tile([P, width], U8, name="b_plane", align_bytes=64)
             nc.vector.quantize_mx(
@@ -347,15 +369,16 @@ def tile_list_pile_loop_readout_kernel(
                         start=True,
                         stop=True,
                     )
-                res = late.tile([P, 2, width], F32, name="res", bufs=6, align_bytes=64)
+                res = late.tile([P, 2, width], F32, name="res", bufs=chunks * OUT_TILES // 2, align_bytes=64)
                 if pair == 1 and c > 0:
                     nc.vector.tensor_copy(out=res[:], in_=acc[:])
                 else:
                     nc.scalar.copy(out=res[:], in_=acc[:])
                 nc.sync.dma_start(out=out_rows[:, 2 * pair : 2 * pair + 2, cols], in_=res[:])
 
-        step_a(0)
-        for half in range(2):
+        w5_codes = keep.tile([P, N], U32, name="w5_codes", tag="look_then_w5_codes", align_bytes=64)
+
+        def quantise_w5(half):
             cols = slice(half * N // 2, (half + 1) * N // 2)
             nc.vector.quantize_mx(
                 out=w5_codes[:, cols].bitcast(E4M3),
@@ -363,7 +386,14 @@ def tile_list_pile_loop_readout_kernel(
                 in_=w5_bf[:, cols, :].rearrange("p c j -> p (c j)"),
             )
 
-        for c in range(chunks):
-            if c + 1 < chunks:
-                step_a(c + 1)
-            step_b(c)
+        for step in range(chunks + 2):
+            if step < chunks:
+                weave(step)
+            if step < 2:
+                quantise_w5(step)
+            else:
+                join(step - 2)
+            if step < chunks:
+                second_stage(step)
+            if step >= 2:
+                third_stage(step - 2)

from contextlib import ExitStack

import concourse.mybir as mybir

K, T, S, NP, H, N = 1024, 4096, 1024, 512, 512, 768
FLOPS = 2 * (3 * K * H * S + H * H * S + H * N * S)

F32 = mybir.dt.float32
BF16 = mybir.dt.bfloat16
I32 = mybir.dt.int32
U32 = mybir.dt.uint32
U16 = mybir.dt.uint16
U8 = mybir.dt.uint8
E4M3 = mybir.dt.float8_e4m3fn_x4
E2M1 = mybir.dt.float4_e2m1fn_x4
ALU = mybir.AluOpType
ACT = mybir.ActivationFunctionType

P = 128
PACK = 4
PASSES = K // (P * PACK)
HALF = 512
EDGES = (0, 128, 384, 640, 896, 1024)
OUT_TILES = N // P


def tile_list_pile_loop_readout_kernel(
    tc, tab_words, tab_scales, offs, pos1, pos2, w1, w2_words, w2_scales, w3, thr, mat, lift, wgs, gain,
    w4_words, w4_scales, gain2, w5, out,
):
    nc = tc.nc

    with ExitStack() as ctx:
        lists = ctx.enter_context(tc.tile_pool(name="lists", bufs=1))
        keep = ctx.enter_context(tc.tile_pool(name="keep", bufs=1))
        psum = ctx.enter_context(tc.psum_pool(name="psum", bufs=8))

        def kept(name, shape, dtype):
            return keep.tile(shape, dtype, name=name, align_bytes=64)

        def bank(shape):
            return psum.tile(shape, F32, name="bank")

        offs_sb = lists.tile([P, S // 16], U16, name="offs_sb")
        pos1_sb = lists.tile([P, NP // 16], U16, name="pos1_sb")
        pos2_sb = lists.tile([P, NP // 16], U16, name="pos2_sb")

        v_words = [[kept(f"v_words{a}{u}", [P, HALF], U32) for u in range(2)] for a in range(PASSES)]
        v_scales = [kept(f"v_scales{a}", [P, S], U8) for a in range(PASSES)]
        w1_codes = [kept(f"w1_codes{a}", [P, H], U32) for a in range(PASSES)]
        w1_scales = [kept(f"w1_scales{a}", [P, H], U8) for a in range(PASSES)]
        w3_codes = [kept(f"w3_codes{a}", [P, H], U32) for a in range(PASSES)]
        w3_scales = [kept(f"w3_scales{a}", [P, H], U8) for a in range(PASSES)]
        w2_codes = kept("w2_codes", [P, PASSES, 2 * H], U8)
        w2_plane = kept("w2_plane", [P, PASSES, H], U8)
        w4_raw = kept("w4_raw", [P, H], I32)
        w4_plane_raw = kept("w4_plane_raw", [P, H], U8)
        w4_codes = kept("w4_codes", [P, H], I32)
        w5_raw = keep.tile([P, PACK, N], F32, name="w5_raw", tag="w5_then_page_bf", align_bytes=64)
        w5_bf = kept("w5_bf", [P, N, PACK], BF16)
        w5_plane = kept("w5_plane", [P, N], U8)
        thr_sb = kept("thr_sb", [P, PACK], F32)
        lift_sb = kept("lift_sb", [P, PACK], F32)
        gain_sb = kept("gain_sb", [P, PACK], F32)
        gain2_sb = kept("gain2_sb", [P, PACK], F32)
        side = kept("side", [P, PACK, S], F32)
        h = [kept(f"h{t}", [P, S], F32) for t in range(PACK)]
        page = [kept(f"page{t}", [P, S], F32) for t in range(PACK)]
        look = [kept(f"look{t}", [P, NP], F32) for t in range(PACK - 1)]
        look.append(keep.tile([P, NP], F32, name="look3", tag="look_then_w5_codes", align_bytes=64))
        mat_sb = [kept(f"mat{u}", [P, 2, NP], F32) for u in range(2)]
        wgs_sb = [
            keep.tile([P, 2, NP], F32, name="wgs0", tag="wgs_then_skip", align_bytes=64),
            kept("wgs1", [P, 2, NP], F32),
        ]
        w1_bf_first = keep.tile([P, PACK, P, PACK], BF16, name="w1_bf0", tag="w1_bf_then_w4_plane", align_bytes=64)

        def stage1(dst_fn, codes, scales, dtype, t):
            width = 2 if dtype is E2M1 else 1
            for u in range(2):
                acc = bank([P, HALF])
                for a in range(PASSES):
                    nc.tensor.matmul_mx(
                        out=acc[:],
                        lhsT=codes(a)[:, width * P * t : width * P * (t + 1)].bitcast(dtype),
                        lhsT_scale=scales(a)[:, P * t : P * (t + 1)],
                        rhs=v_words[a][u][:].bitcast(E4M3),
                        rhs_scale=v_scales[a][:, HALF * u : HALF * (u + 1)],
                        start=(a == 0),
                        stop=(a == PASSES - 1),
                    )
                dst_fn(acc, slice(HALF * u, HALF * (u + 1)))

        with tc.tile_pool(name="early", bufs=1) as early:

            def staged(name, shape, dtype):
                return early.tile(shape, dtype, name=name, align_bytes=64)

            tab_sb = [staged(f"tab{a}", [P, T], I32) for a in range(PASSES)]
            tab_plane = staged("tab_plane", [P, T], U8)
            picked_rows = staged("picked_rows", [P, S], U8)
            w2_raw = staged("w2_raw", [P, PASSES, 2 * H], U8)
            w2_plane_raw = staged("w2_plane_raw", [P, PASSES, H], U8)
            w1_raw = [staged(f"w1_raw{a}", [P, PACK, H], F32) for a in range(PASSES)]
            w3_raw = [staged(f"w3_raw{a}", [P, PACK, H], F32) for a in range(PASSES)]
            w1_bf = [w1_bf_first, staged("w1_bf1", [P, PACK, P, PACK], BF16)]
            w3_bf = [staged(f"w3_bf{a}", [P, PACK, P, PACK], BF16) for a in range(PASSES)]

            nc.vector.memset(tab_plane[0:96].bitcast(I32), 0)
            for a in range(PASSES):
                nc.vector.memset(v_scales[a][:].bitcast(I32), 0)
            nc.gpsimd.memset(w2_plane_raw[:].rearrange("p a c -> p (a c)").bitcast(I32), 0)
            nc.gpsimd.memset(w4_plane_raw[:].bitcast(I32), 0)

            def load_rows(dst, w, a):
                rows = w[a * P * PACK : (a + 1) * P * PACK, :]
                nc.sync.dma_start(out=dst[:], in_=rows.rearrange("(p j) c -> p j c", j=PACK))

            def load_table(a):
                nc.sync.dma_start(out=tab_sb[a][:], in_=tab_words[a].rearrange("p t i -> p (t i)").bitcast(I32))

            nc.sync.dma_start(offs_sb[:], offs)
            nc.sync.dma_start(
                out=tab_plane[96:P].bitcast(I32), in_=tab_scales.rearrange("a q t -> (a q) t").bitcast(I32)
            )
            nc.sync.dma_start(
                out=w2_raw[:].bitcast(I32), in_=w2_words.rearrange("a p c -> p a c").bitcast(I32)
            )
            load_table(0)
            load_table(1)

            for r in range(4):
                nc.gpsimd.dma_start(
                    out=w2_plane_raw[r:P:32].bitcast(I32),
                    in_=w2_scales[:, r:16:4, :].rearrange("a q c -> q a c").bitcast(I32),
                )
            for r in range(4):
                nc.gpsimd.dma_start(
                    out=w4_plane_raw[r:P:32, :].bitcast(I32),
                    in_=w4_scales[0, r:16:4, :].bitcast(I32),
                )
            for dst, vec in ((thr_sb, thr), (lift_sb, lift), (gain_sb, gain), (gain2_sb, gain2)):
                nc.gpsimd.dma_start(out=dst[:], in_=vec.rearrange("(p t) -> p t", t=PACK))

            nc.vector.tensor_copy(out=picked_rows[:], in_=tab_plane[:].indirect(offs_sb[:]))
            for a in range(PASSES):
                for q in range(4):
                    first = 96 + 16 * a + 4 * q
                    nc.scalar.dma_start(
                        out=v_scales[a][32 * q : 32 * q + 4].bitcast(I32), in_=picked_rows[first : first + 4].bitcast(I32)
                    )

            load_rows(w1_raw[0], w1, 0)
            load_rows(w1_raw[1], w1, 1)
            load_rows(w3_raw[0], w3, 0)
            load_rows(w3_raw[1], w3, 1)
            mat_rows = mat.rearrange("(p t) j -> p t j", t=PACK)
            wgs_rows = wgs.rearrange("(q t) j -> q t j", t=PACK)
            nc.sync.dma_start(pos1_sb[:], pos1)
            nc.sync.dma_start(pos2_sb[:], pos2)
            nc.sync.dma_start(out=w4_raw[:], in_=w4_words[0].rearrange("p c i -> p (c i)").bitcast(I32))

            def load_factors(u):
                for q in (0, 2, 1, 3):
                    nc.sync.dma_start(out=wgs_sb[u][32 * q : 32 * q + 32], in_=wgs_rows[:, 2 * u : 2 * u + 2, :])
                nc.sync.dma_start(out=mat_sb[u][:], in_=mat_rows[:, 2 * u : 2 * u + 2, :])

            load_factors(0)
            load_rows(w5_raw, w5, 0)
            load_factors(1)

            def gather_words(a):
                for u in range(2):
                    cols = slice(u * HALF // 16, (u + 1) * HALF // 16)
                    nc.vector.tensor_copy(
                        out=v_words[a][u][:], in_=tab_sb[a][:].bitcast(U32).indirect(offs_sb[:, cols])
                    )

            def deal_views(raw, bf, m0, m1):
                dst = bf[:].rearrange("p t m j -> p m t j")[:, m0:m1]
                src = raw[:].rearrange("p j (m t) -> p m t j", t=PACK)[:, m0:m1]
                return dst, src

            def quantise(bf, codes, scales, t0, t1):
                nc.vector.quantize_mx(
                    out=codes[:, P * t0 : P * t1].bitcast(E4M3),
                    scales=scales[:, P * t0 : P * t1],
                    in_=bf[:, t0:t1].rearrange("p t m j -> p (t m j)"),
                )

            nc.vector.tensor_copy(
                out=w2_codes[:].bitcast(U16).rearrange("p a (t m) -> p a t m", t=PACK),
                in_=w2_raw[:].bitcast(U16).rearrange("p a (m t) -> p a t m", t=PACK),
            )
            nc.vector.tensor_copy(
                out=w2_plane[:].rearrange("p a (t m) -> p a t m", t=PACK),
                in_=w2_plane_raw[:].rearrange("p a (m t) -> p a t m", t=PACK),
            )
            for a in range(PASSES):
                gather_words(a)
            for a in range(PASSES):
                dst, src = deal_views(w1_raw[a], w1_bf[a], 0, P)
                nc.vector.tensor_copy(out=dst, in_=src)
                quantise(w1_bf[a], w1_codes[a], w1_scales[a], 0, PACK)
            w4_plane = keep.tile([P, H], U8, name="w4_plane", tag="w1_bf_then_w4_plane", align_bytes=64)
            nc.vector.tensor_copy(
                out=w4_plane[:].rearrange("p (t m) -> p t m", t=PACK),
                in_=w4_plane_raw[:].rearrange("p (m t) -> p t m", t=PACK),
            )

            for t in range(PACK):
                stage1(
                    lambda acc, cols, t=t: nc.scalar.copy(out=side[:, t, cols], in_=acc[:]),
                    lambda a: w2_codes[:, a, :], lambda a: w2_plane[:, a, :], E2M1, t,
                )

            def larger(t):
                stage1(
                    lambda acc, cols: nc.vector.tensor_tensor(
                        out=side[:, t, cols], in0=acc[:], in1=side[:, t, cols], op=ALU.max
                    ),
                    lambda a: w1_codes[a], lambda a: w1_scales[a], E4M3, t,
                )

            dst, src = deal_views(w3_raw[0], w3_bf[0], 0, P)
            nc.scalar.copy(out=dst, in_=src)
            dst, src = deal_views(w3_raw[1], w3_bf[1], 0, P // 2)
            nc.scalar.copy(out=dst, in_=src)
            dst, src = deal_views(w3_raw[1], w3_bf[1], P // 2, P)
            nc.vector.tensor_copy(out=dst, in_=src)
            for a in range(PASSES):
                quantise(w3_bf[a], w3_codes[a], w3_scales[a], 0, PACK)
            for t in range(PACK):
                larger(t)
        nc.scalar.copy(
            out=w4_codes[:].bitcast(U32).rearrange("p (t m) -> p m t", t=PACK),
            in_=w4_raw[:].bitcast(U32).rearrange("p (m t) -> p m t", t=PACK),
        )

        def features(t):
            stage1(
                lambda acc, cols: nc.vector.tensor_tensor(
                    out=h[t][:, cols], in0=acc[:], in1=side[:, t, cols], op=ALU.mult
                ),
                lambda a: w3_codes[a], lambda a: w3_scales[a], E4M3, t,
            )

        def fetch(t):
            nc.scalar.activation(
                out=look[t][:], in_=h[t][:].indirect(pos1_sb[:]), func=ACT.Sigmoid, bias=thr_sb[:, t : t + 1]
            )

        def fill(t):
            nc.scalar.activation(out=page[t][:], in_=h[t][:], func=ACT.Identity, bias=lift_sb[:, t : t + 1])

        def put(t):
            u, e = divmod(t, 2)
            engine = nc.gpsimd if u == 0 else nc.vector
            engine.tensor_tensor(out=mat_sb[u][:, e, :], in0=mat_sb[u][:, e, :], in1=wgs_sb[u][:, e, :], op=ALU.mult)
            nc.vector.tensor_tensor(
                out=page[t][:].indirect(pos2_sb[:]), in0=look[t][:], in1=mat_sb[u][:, e, :], op=ALU.mult
            )

        for t in range(PACK):
            features(t)
        for t in range(PACK):
            fetch(t)
            fill(t)
        nc.scalar.copy(
            out=w5_bf[:].rearrange("p (c i) j -> p c j i", i=4),
            in_=w5_raw[:].rearrange("p j (c i) -> p c j i", i=4),
        )

        for t in range(PACK):
            put(t)

        late = ctx.enter_context(tc.tile_pool(name="late", bufs=5))
        page_bf = keep.tile([P, PACK, S], BF16, name="page_bf", tag="w5_then_page_bf", align_bytes=64)

        def round_page(t, cols):
            nc.scalar.activation(out=page_bf[:, t, cols], in_=page[t][:, cols], func=ACT.Copy, scale=gain_sb[:, t : t + 1])

        for t in range(PACK - 1):
            round_page(t, slice(0, S))
        skip = keep.tile([P, PACK, S], F32, name="skip", tag="wgs_then_skip", align_bytes=64)
        for t in range(PACK):
            if t < 2:
                nc.gpsimd.tensor_scalar(
                    out=skip[:, t, :], in0=h[t][:], scalar1=gain2_sb[:, t : t + 1], scalar2=0.0,
                    op0=ALU.mult, op1=ALU.add,
                )
            else:
                nc.scalar.activation(out=skip[:, t, :], in_=h[t][:], func=ACT.Copy, scale=gain2_sb[:, t : t + 1])

        out_rows = out.rearrange("(i p) j -> p i j", p=P)
        chunks = len(EDGES) - 1
        state = {}

        def weave(c):
            cols = slice(EDGES[c], EDGES[c + 1])
            width = EDGES[c + 1] - EDGES[c]
            round_page(PACK - 1, cols)
            a_bf = late.tile([P, width, PACK], BF16, name="a_bf", align_bytes=64)
            nc.vector.tensor_copy(
                out=a_bf[:].rearrange("p (c i) t -> p c t i", i=4),
                in_=page_bf[:, :, cols].rearrange("p t (c i) -> p c t i", i=4),
            )
            state["a", c] = a_bf

        def second_stage(c):
            width = EDGES[c + 1] - EDGES[c]
            a_bf = state["a", c]
            a_codes = late.tile([P, width], U32, name="a_codes", align_bytes=64)
            a_plane = late.tile([P, width], U8, name="a_plane", align_bytes=64)
            nc.vector.quantize_mx(
                out=a_codes[:].bitcast(E4M3), scales=a_plane[:], in_=a_bf[:].rearrange("p c t -> p (c t)")
            )
            y = late.tile([P, PACK, width], F32, name="y", align_bytes=64)
            for pair in range(2):
                acc = bank([P, 2, width])
                for e in range(2):
                    t = 2 * pair + e
                    nc.tensor.matmul_mx(
                        out=acc[:, e, :],
                        lhsT=w4_codes[:, P * t : P * (t + 1)].bitcast(E4M3),
                        lhsT_scale=w4_plane[:, P * t : P * (t + 1)],
                        rhs=a_codes[:].bitcast(E4M3),
                        rhs_scale=a_plane[:],
                        start=True,
                        stop=True,
                    )
                for e in range(2):
                    t = 2 * pair + e
                    nc.scalar.activation(out=y[:, t, :], in_=acc[:, e, :], func=ACT.Copy, scale=gain2_sb[:, t : t + 1])
            state["y", c] = y

        def join(c):
            cols = slice(EDGES[c], EDGES[c + 1])
            width = EDGES[c + 1] - EDGES[c]
            y = state["y", c]
            b_bf = late.tile([P, width, PACK], BF16, name="b_bf", align_bytes=64)
            nc.vector.tensor_tensor(
                out=b_bf[:].rearrange("p (c i) t -> p c t i", i=2),
                in0=y[:].rearrange("p t (c i) -> p c t i", i=2),
                in1=skip[:, :, cols].rearrange("p t (c i) -> p c t i", i=2),
                op=ALU.add,
            )
            state["b", c] = b_bf

        def third_stage(c):
            cols = slice(EDGES[c], EDGES[c + 1])
            width = EDGES[c + 1] - EDGES[c]
            b_bf = state["b", c]
            b_codes = late.tile([P, width], U32, name="b_codes", align_bytes=64)
            b_plane = late.tile([P, width], U8, name="b_plane", align_bytes=64)
            nc.vector.quantize_mx(
                out=b_codes[:].bitcast(E4M3), scales=b_plane[:], in_=b_bf[:].rearrange("p c t -> p (c t)")
            )
            for pair in range(OUT_TILES // 2):
                acc = bank([P, 2, width])
                for e in range(2):
                    i = 2 * pair + e
                    nc.tensor.matmul_mx(
                        out=acc[:, e, :],
                        lhsT=w5_codes[:, P * i : P * (i + 1)].bitcast(E4M3),
                        lhsT_scale=w5_plane[:, P * i : P * (i + 1)],
                        rhs=b_codes[:].bitcast(E4M3),
                        rhs_scale=b_plane[:],
                        start=True,
                        stop=True,
                    )
                res = late.tile([P, 2, width], F32, name="res", bufs=chunks * OUT_TILES // 2, align_bytes=64)
                if pair == 1 and c > 0:
                    nc.vector.tensor_copy(out=res[:], in_=acc[:])
                else:
                    nc.scalar.copy(out=res[:], in_=acc[:])
                nc.sync.dma_start(out=out_rows[:, 2 * pair : 2 * pair + 2, cols], in_=res[:])

        w5_codes = keep.tile([P, N], U32, name="w5_codes", tag="look_then_w5_codes", align_bytes=64)

        def quantise_w5(half):
            cols = slice(half * N // 2, (half + 1) * N // 2)
            nc.vector.quantize_mx(
                out=w5_codes[:, cols].bitcast(E4M3),
                scales=w5_plane[:, cols],
                in_=w5_bf[:, cols, :].rearrange("p c j -> p (c j)"),
            )

        for step in range(chunks + 2):
            if step < chunks:
                weave(step)
            if step < 2:
                quantise_w5(step)
            else:
                join(step - 2)
            if step < chunks:
                second_stage(step)
            if step >= 2:
                third_stage(step - 2)
